import numpy as np, ml_dtypes
CORES = [23,119,17,113]
N = 4
BF = ml_dtypes.bfloat16
def gentries(a):
    return np.ascontiguousarray(a.reshape(8, 16, -1).transpose(0, 2, 1)).reshape(8, -1)
def gtable(e):
    e = np.asarray(e); return np.ascontiguousarray(e.reshape(8, -1, 16).transpose(0, 2, 1)).reshape(128, -1).astype(np.int32)
A, S, G, M, W = 2048, 128, 3, 2, 2432
def tabs(e):
    return np.stack([gtable(v.reshape(8, -1)) for v in e])
def alleles(rng, ex):
    return np.minimum(np.floor(256 * rng.random((N, 128, 2 * A), dtype=np.float32) ** ex.astype(np.float32)), 255).astype(BF)
def rivals(rng):
    k = (N, 8, G, M, A)
    return np.where(rng.random(k) < 0.5, rng.integers(0, A, k), rng.integers(A, W, k))
def setup_inputs(rng):
    return {"haps": alleles(rng, np.exp2(2 * rng.random((N, 128, 1)) - 1)), "eff": rng.integers(0, 128, (N, 128, 1)).astype(np.float32).astype(BF),
            "dam": tabs(rng.integers(0, A, (N, 8, G, A))), "rival": tabs(rivals(rng)), "gift": tabs(rng.integers(0, A, (N, 8, G, N - 1, S)))}
def setup_inputs_ties(rng):
    d = setup_inputs(rng); e = rng.integers(0, 2, (N, 8, 16, 1))
    d["haps"] = (254 * rng.integers(0, 2, (1, 128, 1)) + rng.integers(0, 2, (N, 128, 2 * A))).astype(np.float32).astype(BF)
    for r in range(N): e[r, rng.permutation(8)[:3]] = 0
    d["eff"] = e.reshape(N, 128, 1).astype(np.float32).astype(BF)
    v = rivals(rng); v[:, :, :, 1] = np.where(rng.random((N, 8, G, A)) < 0.25, v[:, :, :, 0], v[:, :, :, 1])
    d["rival"] = tabs(v); return d
def edge(rng, e, places):
    return np.where(rng.random(e.shape) < 0.5, rng.choice(np.array(places), e.shape), e)
def setup_inputs_ends(rng):
    d = setup_inputs(rng); d["haps"][:, :, :2] = 255; d["haps"][:, :, 2 * A - 2:] = 0
    e = rng.integers(0, 128, (N, 8, 16, 1))
    for r in range(N): e[r, rng.permutation(8)[:4]] = 127
    d["eff"] = e.reshape(N, 128, 1).astype(np.float32).astype(BF)
    d["dam"] = tabs(edge(rng, rng.integers(0, A, (N, 8, G, A)), [0, A - 1])); d["gift"] = tabs(edge(rng, rng.integers(0, A, (N, 8, G, N - 1, S)), [0, A - 1]))
    d["rival"] = tabs(edge(rng, rivals(rng), [0, A - 1] + [A + S * k for k in range(N - 1)] + [A + S * k + S - 1 for k in range(N - 1)])); return d
def setup_inputs_one(rng):
    d = setup_inputs(rng); a = rng.integers(0, A, (N, 8, G, A)); a[:, :, 0] = rng.integers(0, A, (N, 8, 1))
    v = rivals(rng); v[:, :, :, 0] = rng.integers(0, W, (N, 8, G, 1))
    b = np.zeros((N, 8, G, N - 1, S), np.int64); b[:] = rng.integers(0, A, (N, 8, G, N - 1, 1))
    d["dam"] = tabs(a); d["rival"] = tabs(v); d["gift"] = tabs(b); return d
def setup_inputs_guests(rng):
    d = setup_inputs(rng)
    v = np.zeros((N, 8, G, M * A), np.int64); v[:] = np.arange(M * A) % (W - A); d["rival"] = tabs(A + rng.permuted(v, axis=-1))
    a = np.zeros((N, 8, G, A), np.int64); a[:] = np.arange(A); d["dam"] = tabs(rng.permuted(a, axis=-1))
    b = np.zeros((N, 8, G, N - 1, A), np.int64); b[:] = np.arange(A); d["gift"] = tabs(rng.permuted(b, axis=-1)[..., :S]); return d
def setup_inputs_spread(rng):
    d = setup_inputs(rng); d["haps"] = alleles(rng, np.exp2(8 * rng.random((N, 128, 1)) - 4))
    d["eff"] = np.floor(128 * rng.random((N, 128, 1)) ** 4).astype(np.float32).astype(BF)
    def u(m, *k): return np.minimum((m * rng.random(k) ** 3).astype(np.int64), m - 1)
    k = (N, 8, G, M, A)
    d["dam"] = tabs(A - 1 - u(A, N, 8, G, A)); d["gift"] = tabs(u(A, N, 8, G, N - 1, S))
    d["rival"] = tabs(np.where(rng.random(k) < 0.5, u(A, *k), W - 1 - u(W - A, *k))); return d
def check_inputs(d):
    bad = []
    h = d["haps"].astype(np.float32); e = d["eff"].astype(np.float32)
    if not ((h >= 0) & (h <= 255) & (h == np.floor(h))).all(): bad.append("haps: whole numbers from 0 to 255")
    if not ((e >= 0) & (e <= 127) & (e == np.floor(e))).all(): bad.append("eff: whole numbers from 0 to 127")
    for k, top in (("dam", A), ("rival", W), ("gift", A)):
        if not ((d[k] >= 0) & (d[k] < top)).all(): bad.append(k + ": range")
    return bad
def reference(haps, eff, dam, rival, gift):
    h = haps.astype(np.int32).reshape(N, 8, 16, A, 2); e = eff.astype(np.int32).reshape(N, 8, 16, 1)
    dl = np.stack([gentries(a) for a in dam]).reshape(N, 8, G, A)
    rl = np.stack([gentries(a) for a in rival]).reshape(N, 8, G, M, A)
    gl = np.stack([gentries(a) for a in gift]).reshape(N, 8, G, N - 1, S)
    i = np.arange(A); mk = np.arange(16)[:, None]
    for t in range(G):
        new = np.zeros_like(h)
        for r in range(N):
            parts = [h[r]]
            for d in range(N - 1):
                q = (r - 1 - d) % N
                parts.append(np.take_along_axis(h[q], gl[q, :, t, d][:, None, :, None], 2))
            w = np.concatenate(parts, 2)
            v = np.sum(e[r] * (w[..., 0] + w[..., 1]), axis=1)
            best = rl[r, :, t, 0]
            for m in range(1, M):
                c = rl[r, :, t, m]; vb = np.take_along_axis(v, best, 1); vc = np.take_along_axis(v, c, 1)
                best = np.where((vc > vb) | ((vc == vb) & (c > best)), c, best)
            for k, p in enumerate((dl[r, :, t], best)):
                x = (181 * p + 75 * i + 217 * t + 389 * k) & 1023
                s = (x >> 9)[:, None]; c = ((x >> 5) & 15)[:, None]
                side = np.where(mk < c, s, 1 - s)
                both = np.take_along_axis(w, p[:, None, :, None], 2)
                new[r, ..., k] = np.take_along_axis(both, side[..., None], 3)[..., 0]
        h = new
    return {"y": h.reshape(N, 128, 2 * A).astype(BF)}

from concourse.bass import DstId, RemoteDMATransfer
from concourse.mybir import AluOpType, ActivationFunctionType

A, S, G, NR = 2048, 128, 3, 4
W = A + (NR - 1) * S
Q = 512
ZS = 16384.0
HALF = 127.5

SCRATCH = {
    "hp": ("sbuf", [128, 2 * A], "bfloat16"),
    "ef": ("sbuf", [128, 16], "bfloat16"),
    "dami": ("sbuf", [128, 384], "int32"),
    "rivi": ("sbuf", [128, 768], "int32"),
    "gfi": ("sbuf", [128, 72], "int32"),
    "ci": ("sbuf", [128, 128], "int32"),
    "jt": ("sbuf", [128, 384], "int32"),
    "sh": ("sbuf", [128, 8], "int32"),
    "mtmp": ("sbuf", [128, 32], "int32"),
    "mt": ("sbuf", [128, 32], "bfloat16"),
    "idh": ("sbuf", [128, 128], "bfloat16"),
    "id1": ("sbuf", [128, 128], "bfloat16"),
    "bb": ("sbuf", [128, 144], "bfloat16"),
    "kk": ("sbuf", [128, 64], "bfloat16"),
    "col": ("sbuf", [128, 8], "float32"),
    "gos": ("sbuf", [128, 72], "uint16"),
    "god": ("sbuf", [128, 72], "uint16"),
    "dx1": ("sbuf", [128, 384], "float32"),
    "dx2": ("sbuf", [128, 384], "int32"),
    "dx3": ("sbuf", [128, 384], "int32"),
    "du": ("sbuf", [128, 384], "uint16"),
    "dos": ("sbuf", [128, 384], "uint16"),
    "dod": ("sbuf", [128, 384], "uint16"),
    "rlo": ("sbuf", [128, 384], "float32"),
    "rhi": ("sbuf", [128, 384], "float32"),
    "olo": ("sbuf", [128, 384], "uint16"),
    "ohi": ("sbuf", [128, 384], "uint16"),
    "s2": ("sbuf", [128, 384], "float32"),
    "sx2": ("sbuf", [128, 384], "int32"),
    "sx3": ("sbuf", [128, 384], "int32"),
    "su": ("sbuf", [128, 384], "uint16"),
    "sos": ("sbuf", [128, 384], "uint16"),
    "sod": ("sbuf", [128, 384], "uint16"),
    "yy": ("sbuf", [128, 2 * A], "bfloat16"),
    "pz0": ("psum", [128, 512], "float32"),
    "pz1": ("psum", [128, 512], "float32"),
}
for _t in range(G):
    SCRATCH["x%d" % _t] = ("sbuf", [128, 2 * W], "bfloat16")
    SCRATCH["gb%d" % _t] = ("sbuf", [128, 2 * (W - A)], "bfloat16")
    for _n in ("md", "ms", "vh", "vl", "td", "ts", "ed", "es"):
        SCRATCH["%s%d" % (_n, _t)] = ("sbuf", [128, A], "bfloat16")
for _q in range(6):
    SCRATCH["pt%d" % _q] = ("psum", [128, 512], "float32")

SEMAPHORES = (["cv", "ca", "cp", "cg", "lgf", "lef", "ld0", "ld1", "lr0", "lr1"] + ["lh%d" % q for q in range(4)]
              + ["arr%d" % t for t in range(G)] + ["snt%d" % t for t in range(G)] + ["st%d" % q for q in range(4)])

DAM_PE = {(0, 0): 4, (0, 1): 5, (1, 0): 4, (1, 1): 5, (2, 0): 4, (2, 1): 5, (2, 2): 2, (2, 3): 3}
SIRE_V = ((2, 2), (2, 3))
D_FIRST = (3,)
ORDER = {
    "v": "k_m1 k_bz k_sh k_id k_kk k_i1 k_c0 k_m2 dx1_0 dx2_0 dx3_0 du_0 dos_0 dx1_2 dx1_1 sv_0_0 dx2_1 dos_1 dod_2 dx2_2 dod_0 "
         "dos_2 dv_0_0 dv_0_1 god gos dv_0_3 dv_0_2 dx3_1 gs_0 rh_0 rl_0 rh_1 ol_0 td_0_0 du_1 oh_0 k_b td_0_123 rh_2 ge_0_23 "
         "vh_0_0 vl_0_1 oh_1 rl_1 vh_0_3 dod_1 c1_0_0 k_c1 c2_0_0 os_0_0 x1_0_0 dx3_2 x2_0_0 x3_0_0 du_2 xu_0_0 c1_0_1 c2_0_1 "
         "od_0_0 x1_0_1 os_0_1 x2_0_1 od_0_1 x3_0_1 tm_0_1 xu_0_1 tm_0_0 ss_0_2 tm_0_2 tm_0_3 dv_1_1 dv_1_0 oh_2 dv_1_3 dv_1_2 "
         "ol_1 gd_1 td_1_123 md_2_3 td_1_0 ge_1_2 vh_1_0 vl_1_1 vh_1_3 c1_1_0 c2_1_0 x1_1_0 x2_1_0 os_1_0 x3_1_0 xu_1_0 ge_1_3 "
         "c1_1_1 c2_1_1 od_1_0 x1_1_1 os_1_1 x2_1_1 tm_1_0 x3_1_1 od_1_1 xu_1_1 tm_1_1 ms_1_3 tm_1_2 tm_1_3 dv_2_0 dv_2_3 dv_2_1 "
         "dv_2_2 gd_2 td_2_01 rl_2 td_2_23 ol_2 sd_2_2 vh_2_0 vl_2_0 vh_2_2 c1_2_0 c2_2_0 x1_2_0 os_2_0 x2_2_0 x3_2_0 od_2_0 "
         "xu_2_0 ss_2_0 c1_2_1 c2_2_1 x1_2_1 tm_2_0 x2_2_1 x3_2_1 xu_2_1 tm_2_1 od_2_1 os_2_1 tm_2_2 gf_2_2 tm_2_3 gf_2_3 yb_3",
    "a": "md_0_01 sv_0_1 sv_0_2 md_0_2 sv_0_3 gd_0 md_0_3 sd_0_01 md_1_0123 vh_0_1 vl_0_0 vh_0_2 vl_0_23 ss_0_1 ms_0_1 ms_0_0 "
         "ss_0_0 ms_0_2 ms_0_3 sv_1_1 sv_1_0 ss_0_3 sv_1_2 sv_1_3 gs_1 sd_1_01 md_2_012 vh_1_1 vl_1_0 vh_1_2 vl_1_23 ms_1_0 "
         "ms_1_1 ss_1_01 ms_1_2 ss_1_3 sv_2_0 ss_1_2 sv_2_1 sv_2_2 sv_2_3 gs_2 sd_2_01 sd_2_3 ya_1 ya_0 vh_2_1 vl_2_1 vh_2_3 "
         "vl_2_23 ms_2_0 ms_2_1 ss_2_1 ms_2_2 yb_0 ms_2_3 yb_1 ya_2 yb_2 ya_3",
    "p": "in_0_0 in_0_1 in_0_2 in_0_3 ea_0_0 te_1_0 te_1_1 te_1_3 za_0_0 z_0_0 za_0_1 z_0_1 ea_0_1 te_1_2 tg_1_1 tf_1_1 tg_1_0 "
         "tf_1_0 tg_1_2 tf_1_2 tg_1_3 tf_1_3 ea_1_1 te_2_1 te_2_0 za_1_0 z_1_0 za_1_1 z_1_1 te_2_3 ea_1_0 tg_2_0 tf_2_0 tg_2_1 "
         "te_2_2 tf_2_1 tg_2_2 tg_2_3 tf_2_3 tf_2_2 ea_2_1 ea_2_0 za_2_0 z_2_0 za_2_1 z_2_1 ea_2_2 tg_3_0 tf_3_0 tg_3_1 tf_3_1 "
         "ea_2_3",
    "g": "i_ci i_jt send_0 send_1 send_2",
    "s": "l_d0 l_h0 l_d1 l_h1 l_h2 l_h3 l_gf l_r0 l_ef l_r1 st_0 st_1 st_2 st_3",
}
GATHERS = ("md", "td", "ge", "sd", "vh", "vl", "ms", "tm", "ss", "gf")


def nm(base, t, qs):
    return ["%s_%d_%d" % (base, t, q) for q in qs]


def rank_program(g, core, T, topo):
    rank = T.rank_of(core)
    if rank is None:
        return
    ALU, ACT = AluOpType, ActivationFunctionType
    vec, act, pe = g.vector, g.scalar, g.tensor
    queue = {"v": vec, "a": act, "p": pe, "s": g.sync, "g": g}
    order = {e: ORDER[e].split() for e in ORDER}
    where, alias, spans = {}, {}, {}
    for e in order:
        for n in order[e]:
            where[n] = e
            p = n.split("_")
            if p[0] in GATHERS:
                qs = [int(c) for c in p[2]]
                spans.setdefault((p[0], int(p[1])), []).append((n, qs))
                for q in qs:
                    alias["%s_%s_%d" % (p[0], p[1], q)] = n
    ops = {}

    def add(name, deps, fn, sem=None, inc=1, after=()):
        ops[name] = ([alias.get(d, d) for d in deps], fn, sem, inc, list(after))

    def ts(out, in0, s1, op0, s2=None, op1=None):
        if op1 is None:
            return vec.tensor_scalar(out, in0, s1, None, op0)
        return vec.tensor_scalar(out, in0, s1, s2, op0, op1)

    def affine(name, out, in_, scale, bias):
        if where[name] == "a":
            if bias == 0.0:
                return act.activation(out, in_, ACT.Copy, scale=scale)
            return act.activation(out, in_, ACT.Identity, bias=bias, scale=scale)
        if scale == 1.0 and bias == 0.0:
            return vec.tensor_copy(out, in_)
        return ts(out, in_, scale, ALU.mult, bias, ALU.add)

    def mms(out, terms, start, stop):
        def run():
            ins = None
            for k, (lhs, rhs) in enumerate(terms):
                ins = pe.matmul(out, lhs, rhs, start and k == 0, stop and k == len(terms) - 1)
            return ins
        return run

    def load(name, sem, out, in_):
        add(name, [], lambda: queue[where[name]].dma_start(out, in_), sem, 16)

    load("l_gf", "lgf", T.gfi[:, :], T.gift[:, :])
    load("l_ef", "lef", T.ef[:, 0:1], T.eff[:, :])
    load("l_d0", "ld0", T.dami[:, 0:128], T.dam[:, 0:128])
    load("l_d1", "ld1", T.dami[:, 128:384], T.dam[:, 128:384])
    load("l_r0", "lr0", T.rivi[:, 0:256], T.rival[:, 0:256])
    load("l_r1", "lr1", T.rivi[:, 256:768], T.rival[:, 256:768])
    for q in range(4):
        load("l_h%d" % q, "lh%d" % q, T.hp[:, 2 * Q * q:2 * Q * (q + 1)], T.haps[:, 2 * Q * q:2 * Q * (q + 1)])

    add("i_ci", [], lambda: g.iota(T.ci[:, :], [[1, 128]], 255, -1))
    add("i_jt", [], lambda: g.iota(T.jt[:, :], [[217, G], [75 * 16, 128]], 0, 75))
    add("k_kk", [], lambda: vec.memset(T.kk[:, :], 8192.0))
    add("k_bz", [], lambda: vec.memset(T.bb[:, :], 0.0))
    add("k_sh", ["i_ci"], lambda: ts(T.sh[:, :], T.ci[:, 0:128:16], 4, ALU.arith_shift_right))
    add("k_id", ["i_ci"], lambda: ts(T.idh[:, :], T.ci[:, :], 255.0, ALU.is_equal, 0.5, ALU.mult))
    add("k_i1", ["i_ci"], lambda: ts(T.id1[:, :], T.ci[:, :], 255.0, ALU.is_equal))
    add("k_m1", ["i_ci"], lambda: ts(T.mtmp[:, :], T.ci[:, 0:32], 16, ALU.bitwise_and))
    add("k_m2", ["k_m1"], lambda: ts(T.mt[:, :], T.mtmp[:, :], -0.125, ALU.mult, 1.0, ALU.add))
    for b in range(2):
        add("k_c%d" % b, ["k_sh"], lambda b=b: ts(T.col[:, b:b + 1], T.sh[:, 0:1], 688.0, ALU.mult, 944.0 + 389.0 * b, ALU.add))
    add("k_b", ["k_sh", "k_bz", "l_ef"], lambda: ts(T.bb[:, 15:128:16], T.sh[:, :], 15.0, ALU.is_equal, T.ef[:, 0:1], ALU.mult))
    idh, id1 = T.idh[:, :], T.id1[:, :]

    add("gos", ["l_gf"], lambda: ts(T.gos[:, :], T.gfi[:, :], 2.0, ALU.mult))
    add("god", ["l_gf"], lambda: ts(T.god[:, :], T.gfi[:, :], 2.0, ALU.mult, 1.0, ALU.add))
    for t in range(G):
        ld, c = "l_d%d" % min(t, 1), slice(128 * t, 128 * t + 128)
        add("dx1_%d" % t, [ld, "k_c0"], lambda c=c: ts(T.dx1[:, c], T.dami[:, c], 181.0, ALU.mult, T.col[:, 0:1], ALU.add))
        add("dx2_%d" % t, ["dx1_%d" % t, "i_jt"], lambda c=c: vec.tensor_tensor(T.dx2[:, c], T.dx1[:, c], T.jt[:, c], ALU.add))
        add("dx3_%d" % t, ["dx2_%d" % t], lambda c=c: ts(T.dx3[:, c], T.dx2[:, c], 5, ALU.arith_shift_right, 31, ALU.bitwise_and))
        add("du_%d" % t, ["dx3_%d" % t], lambda c=c: vec.tensor_copy(T.du[:, c], T.dx3[:, c]))
        add("dos_%d" % t, [ld], lambda c=c: ts(T.dos[:, c], T.dami[:, c], 2.0, ALU.mult))
        add("dod_%d" % t, [ld], lambda c=c: ts(T.dod[:, c], T.dami[:, c], 2.0, ALU.mult, 1.0, ALU.add))

    def engine_sets(r):
        src, to = T.cores[r], [T.cores[(r + 1 + d) % NR] for d in range(NR - 1)]
        far = [c for c in to if topo.chip(c) != topo.chip(src)]
        sets, used = {}, []
        for k, c in enumerate(far):
            pool = topo.engines(src, c)
            n = 1
            while 2 * n * len(far) <= len(pool):
                n *= 2
            sets[c] = pool[k * n:(k + 1) * n]
            used += sets[c]
        for c in to:
            if c not in far:
                sets[c] = [e for e in topo.engines(src, c) if e not in used][:4]
                used += sets[c]
        return sets

    dsts = [T.cores[(rank + 1 + d) % NR] for d in range(NR - 1)]
    mine = engine_sets(rank)
    sent = sum(len(mine[c]) for c in dsts)
    arrive = sum(len(engine_sets(r)[core]) for r in range(NR) if r != rank)

    def send(t):
        tr = []
        for d, c in enumerate(dsts):
            rid, pid = topo.addr(c)[:2]
            tr.append(RemoteDMATransfer(dst_ids=[DstId(rid=rid, pnc=pid)], dma_engine_mask=sum(1 << e for e in mine[c]),
                                        remote_sem=T.sem["arr%d" % t], src=T["gb%d" % t][:, 2 * S * d:2 * S * (d + 1)],
                                        dst=T["x%d" % t][:, 2 * A + 2 * S * d:2 * A + 2 * S * (d + 1)]))
        return g.remote_dma_fused(tr, local_sem=T.sem["snt%d" % t])

    def generation(t):
        X, last = T["x%d" % t], t == G - 1
        own = nm("sv", t, range(4)) + nm("dv", t, range(4))
        full = own + ["arr_%d" % t]
        md, ms, vh, vl = T["md%d" % t], T["ms%d" % t], T["vh%d" % t], T["vl%d" % t]
        td, tm, ed, es, gb = T["td%d" % t], T["ts%d" % t], T["ed%d" % t], T["es%d" % t], T["gb%d" % t]
        xo, xw, mt = X[:, 0:2 * A], X[:, :], T.mt[:, :]

        def cols(qs):
            return slice(Q * qs[0], Q * (qs[-1] + 1))

        def offs(qs):
            return slice(128 * t + 32 * qs[0], 128 * t + 32 * (qs[-1] + 1))

        def halves(b, qs):
            return ["%s_%d_%d" % (b, t, h) for h in sorted(set(q // 2 for q in qs))]

        def gather(step, deps, out, win, off, scale=1.0):
            for n, qs in spans.get((step, t), []):
                add(n, deps(qs), lambda n=n, qs=qs: affine(n, out[:, cols(qs)], win.indirect(off[:, offs(qs)]), scale, 0.0))

        def gather2(step, deps, out, win, off, other, op):
            for n, qs in spans.get((step, t), []):
                add(n, deps(qs), lambda qs=qs: vec.tensor_tensor(out[:, cols(qs)], win.indirect(off[:, offs(qs)]), other[:, cols(qs)], op))

        for q in range(4):
            P, u = T["pt%d" % q][:, :], "_%d_%d" % (t, q)
            xs, xd = X[:, 2 * Q * q:2 * Q * (q + 1):2], X[:, 2 * Q * q + 1:2 * Q * (q + 1):2]
            if t == 0:
                dam = T.hp[:, 2 * Q * q:2 * Q * (q + 1):2]
                add("in" + u, ["k_id", "l_h%d" % q], mms(P, [(idh, dam), (idh, T.hp[:, 2 * Q * q + 1:2 * Q * (q + 1):2])], True, True))
                made, bias = "in" + u, -HALF
            else:
                dam, made, bias = T["ed%d" % (t - 1)][:, cols([q])], "tf" + u, 0.0
            if (t - 1, q) in DAM_PE:
                add("sv" + u, [made], lambda u=u, xs=xs, P=P, bias=bias: affine("sv" + u, xs, P, 1.0, bias))
                add("dv" + u, ["sv" + u, "ea_%d_%d" % (t - 1, q)],
                    lambda xd=xd, xs=xs, E=T["pt%d" % DAM_PE[t - 1, q]][:, :]: vec.tensor_tensor(xd, E, xs, ALU.subtract))
            else:
                first = q in D_FIRST
                add("sv" + u, [made] + (["dv" + u] if first else []), lambda u=u, xs=xs, P=P, bias=bias: affine("sv" + u, xs, P, 1.0, bias))
                add("dv" + u, [made] + ([] if first else ["sv" + u]), lambda xd=xd, dam=dam, P=P: vec.tensor_tensor(xd, dam, P, ALU.subtract))
        for n, off, o in (("gs_%d" % t, "gos", 0), ("gd_%d" % t, "god", 1)):
            add(n, own + [off], lambda n=n, off=off, o=o: affine(n, gb[:, o:2 * (W - A):2], xo.indirect(T[off][:, 24 * t:24 * t + 24]), 1.0, 0.0))
        add("send_%d" % t, ["gs_%d" % t, "gd_%d" % t], lambda: send(t), "snt%d" % t, -sent)
        gather("md", lambda qs: ["du_%d" % t, "k_m2"], md, mt, T.du)
        gather2("td", lambda qs: own + ["dod_%d" % t] + nm("md", t, qs), td, xo, T.dod, md, ALU.mult)
        gather2("ge", lambda qs: own + ["dos_%d" % t] + nm("td", t, qs), ed, xo, T.dos, td, ALU.add)
        gather("sd", lambda qs: own + ["dos_%d" % t], ed, xo, T.dos)
        cl, lr = slice(128 * t, 128 * t + 128), "l_r%d" % min(t, 1)
        r0, r1 = T.rivi[:, 256 * t:256 * t + 128], T.rivi[:, 256 * t + 128:256 * t + 256]
        add("rl_%d" % t, [lr], lambda: vec.tensor_tensor(T.rlo[:, cl], r0, r1, ALU.min))
        add("rh_%d" % t, [lr], lambda: vec.tensor_tensor(T.rhi[:, cl], r0, r1, ALU.max))
        add("ol_%d" % t, ["rl_%d" % t], lambda: ts(T.olo[:, cl], T.rlo[:, cl], 2.0, ALU.mult))
        add("oh_%d" % t, ["rh_%d" % t], lambda: ts(T.ohi[:, cl], T.rhi[:, cl], 2.0, ALU.mult))
        gather("vh", lambda qs: full + ["oh_%d" % t], vh, xw, T.ohi, ZS)
        gather("vl", lambda qs: full + ["ol_%d" % t], vl, xw, T.olo, -ZS)
        for h in range(2):
            o, u, Z = slice(128 * t + 64 * h, 128 * t + 64 * h + 64), "_%d_%d" % (t, h), T["pz%d" % h]
            pick = [[(T.bb[:, 15 - r:143 - r], b[:, 1024 * h + r:1024 * (h + 1):16]) for r in range(16)] for b in (vh, vl)]
            add("za" + u, ["k_id", "k_kk", "k_b"] + nm("vh", t, (2 * h, 2 * h + 1)) + (["x2_%d_%d" % (t - 1, h)] if t else []),
                mms(Z[:, 0:64], [(idh, T.kk[:, :])] + pick[0], True, False), None, 0)
            add("z" + u, nm("vl", t, (2 * h, 2 * h + 1)), mms(Z[:, 0:64], pick[1], False, True), after=["za" + u])
            add("c1" + u, ["z" + u, "rl_%d" % t], lambda o=o, Z=Z: vec.tensor_tensor(Z[:, 64:128], Z[:, 0:64], T.rlo[:, o], ALU.max))
            add("c2" + u, ["c1" + u, "rh_%d" % t], lambda o=o, Z=Z: vec.tensor_tensor(T.s2[:, o], Z[:, 64:128], T.rhi[:, o], ALU.min))
            add("x1" + u, ["c2" + u, "k_c1"], lambda o=o, Z=Z: ts(Z[:, 128:192], T.s2[:, o], 181.0, ALU.mult, T.col[:, 1:2], ALU.add))
            add("x2" + u, ["x1" + u, "i_jt"], lambda o=o, Z=Z: vec.tensor_tensor(T.sx2[:, o], Z[:, 128:192], T.jt[:, o], ALU.add))
            add("x3" + u, ["x2" + u], lambda o=o: ts(T.sx3[:, o], T.sx2[:, o], 5, ALU.arith_shift_right, 31, ALU.bitwise_and))
            add("xu" + u, ["x3" + u], lambda o=o: vec.tensor_copy(T.su[:, o], T.sx3[:, o]))
            add("os" + u, ["c2" + u], lambda o=o: ts(T.sos[:, o], T.s2[:, o], 2.0, ALU.mult))
            add("od" + u, ["c2" + u], lambda o=o: ts(T.sod[:, o], T.s2[:, o], 2.0, ALU.mult, 1.0, ALU.add))
        gather("ms", lambda qs: halves("xu", qs) + ["k_m2"], ms, mt, T.su)
        gather2("tm", lambda qs: full + halves("od", qs) + nm("ms", t, qs), tm, xw, T.sod, ms, ALU.mult)
        gather2("gf", lambda qs: full + halves("os", qs) + nm("tm", t, qs), es, xw, T.sos, tm, ALU.add)
        gather("ss", lambda qs: full + halves("os", qs), es, xw, T.sos)
        for q in range(4):
            P, c, u, un = T["pt%d" % q][:, :], cols([q]), "_%d_%d" % (t, q), "_%d_%d" % (t + 1, q)
            onpe, onv = (t, q) in DAM_PE, (t, q) in SIRE_V
            if onpe:
                E = T["pt%d" % DAM_PE[t, q]][:, :]
                add("ea" + u, own + ["k_i1", "sd" + u, "td" + u], mms(E, [(id1, ed[:, c]), (id1, td[:, c])], True, True))
            if not last:
                add("te" + un, own + (["sd" + u, "td" + u] if onpe else ["ge" + u]),
                    mms(P, [(idh, ed[:, c])] + ([(idh, td[:, c])] if onpe else []), True, False), None, 0)
                if onv:
                    add("tf" + un, ["gf" + u], mms(P, [(idh, es[:, c])], False, True), after=["te" + un])
                else:
                    add("tg" + un, ["tm" + u], mms(P, [(idh, tm[:, c])], False, False), None, 0, ["te" + un])
                    add("tf" + un, ["ss" + u], mms(P, [(idh, es[:, c])], False, True), after=["tg" + un])
                continue
            ya, yb = T.yy[:, 2 * Q * q:2 * Q * (q + 1):2], T.yy[:, 2 * Q * q + 1:2 * Q * (q + 1):2]
            add("ya_%d" % q, ["ea" + u if onpe else "ge" + u], lambda q=q, ya=ya, src=(E if onpe else ed[:, c]): affine("ya_%d" % q, ya, src, 1.0, HALF))
            if not onv:
                add("tg" + un, own + ["k_i1", "tm" + u], mms(P, [(id1, tm[:, c])], True, False), None, 0)
                add("tf" + un, ["ss" + u], mms(P, [(id1, es[:, c])], False, True), after=["tg" + un])
            add("yb_%d" % q, ["gf" + u if onv else "tf" + un], lambda q=q, yb=yb, src=(es[:, c] if onv else P): affine("yb_%d" % q, yb, src, 1.0, HALF))
            add("st_%d" % q, ["ya_%d" % q, "yb_%d" % q],
                lambda q=q: queue[where["st_%d" % q]].dma_start(T.y[:, 2 * Q * q:2 * Q * (q + 1)], T.yy[:, 2 * Q * q:2 * Q * (q + 1)]), "st%d" % q, 16)

    for t in range(G):
        generation(t)
    assert sorted(ops) == sorted(where)

    count = {"arr%d" % t: arrive for t in range(G)}
    done = {"arr_%d" % t: ("arr%d" % t, arrive, {}) for t in range(G)}
    known = {e: {} for e in order}

    def wait(e, deps):
        need = {}
        for d in deps:
            sem, val, clock = done[d]
            if known[e].get(sem, 0) < val and need.get(sem, (0, None))[0] < val:
                need[sem] = (val, clock)
        for sem in sorted(need, key=lambda x: -sum(need[x][1].values())):
            val, clock = need[sem]
            if known[e].get(sem, 0) < val:
                queue[e].wait_ge(T.sem[sem], val)
                known[e][sem] = val
            for k in clock:
                known[e][k] = max(known[e].get(k, 0), clock[k])

    pos = {e: 0 for e in order}
    left = sum(len(order[e]) for e in order)
    while left:
        moved = False
        for e in order:
            while pos[e] < len(order[e]):
                name = order[e][pos[e]]
                deps, fn, sem, inc, after = ops[name]
                if not all(d in done for d in deps):
                    break
                assert all(d in done for d in after)
                wait(e, deps)
                ins = fn()
                sem = sem or "c" + e
                if inc > 0:
                    ins.then_inc(T.sem[sem], inc)
                count[sem] = count.get(sem, 0) + abs(inc)
                done[name] = (sem, count[sem], dict(known[e]))
                pos[e] += 1
                left -= 1
                moved = True
        assert moved
    for sem in sorted(count, key=lambda x: x.startswith("st")):
        if count[sem] and max(known[e].get(sem, 0) for e in known) < count[sem]:
            g.wait_ge(T.sem[sem], count[sem])
